import numpy as np
import ml_dtypes

BF16 = ml_dtypes.bfloat16


def bf(x):
    return np.asarray(x, np.float32).astype(BF16)


def f32(x):
    return np.asarray(x, np.float32)


def f64(x):
    return np.asarray(x).astype(np.float64)


def striped(idx):
    return np.tile(idx.reshape(-1, 16).T, (8, 1))


S, K, M, N, B, Q = 256, 128, 128, 192, 2, 96


def setup_inputs():
    return {"base": bf(np.random.standard_normal((B, M, S))), "x": bf(np.random.standard_normal((K, N))), "w": bf(np.random.standard_normal((K, M)) / np.sqrt(K)), "b": f32(0.5 * np.random.standard_normal((M, 1))), "offs": striped(np.random.permutation(S)[:N])}


def reference(base, x, w, b, offs):
    idx = offs[:16].T.reshape(-1)
    z = f64(base).copy()
    for i in range(B):
        z[i][:, idx[i * Q : (i + 1) * Q]] = f64(w).T @ f64(x)[:, i * Q : (i + 1) * Q]
    return np.maximum(z + f64(b), 0.0)

@@ -1,0 +1,57 @@
+import concourse.mybir as mybir
+from concourse.masks import make_identity
+
+BF16, F32, U16 = mybir.dt.bfloat16, mybir.dt.float32, mybir.dt.uint16
+ADD, MAX = mybir.AluOpType.add, mybir.AluOpType.max
+RELU = mybir.ActivationFunctionType.Relu
+
+P = 128
+TOKENS = 256
+ENTRIES = 192
+SEQUENCES = 2
+PIECE = ENTRIES // SEQUENCES
+PIECE_COLUMNS = PIECE // 16
+
+FLOPS = 2 * P * P * ENTRIES
+
+
+def tile_scatter_matmul_kernel(tc, base, x, w, b, offs, out):
+    nc = tc.nc
+    with (
+        tc.tile_pool(name="held", bufs=1) as held,
+        tc.psum_pool(name="windows", bufs=1) as windows,
+    ):
+        offsets = held.tile([P, ENTRIES // 16], U16, name="offsets")
+        nc.sync.dma_start(offsets[:], offs)
+        base_tiles = [held.tile([P, TOKENS], BF16, name=f"base{i}") for i in range(SEQUENCES)]
+        nc.scalar.dma_start(base_tiles[0][:], base[0])
+        nc.sync.dma_start(base_tiles[1][:], base[1])
+        weights = held.tile([P, P], BF16, name="weights")
+        nc.scalar.dma_start(weights[:], w)
+        moving = held.tile([P, ENTRIES], BF16, name="moving")
+        nc.sync.dma_start(moving[:], x)
+        bias = held.tile([P, 1], F32, name="bias")
+        nc.scalar.dma_start(bias[:], b)
+
+        identity = held.tile([P, P], BF16, name="identity")
+        make_identity(nc, identity[:])
+
+        window = [windows.tile([P, TOKENS], F32, name=f"window{i}") for i in range(SEQUENCES)]
+        for i in range(SEQUENCES):
+            nc.tensor.matmul(window[i][:], identity[:], base_tiles[i][:], start=True, stop=True)
+
+        for i in range(SEQUENCES):
+            piece = offsets[:, i * PIECE_COLUMNS : (i + 1) * PIECE_COLUMNS]
+            nc.tensor.matmul(
+                window[i][:].indirect(piece),
+                weights[:],
+                moving[:, i * PIECE : (i + 1) * PIECE],
+                start=True,
+                stop=True,
+            )
+
+        result = [held.tile([P, TOKENS], F32, name=f"result{i}") for i in range(SEQUENCES)]
+        nc.vector.tensor_scalar(result[0][:], window[0][:], bias[:, 0:1], 0.0, ADD, MAX)
+        nc.sync.dma_start(out[0], result[0][:])
+        nc.scalar.activation(result[1][:], window[1][:], RELU, bias=bias[:, 0:1])
+        nc.scalar.dma_start(out[1], result[1][:])

@@ -3,7 +3,6 @@ from concourse.masks import make_identity
 
 BF16, F32, U16 = mybir.dt.bfloat16, mybir.dt.float32, mybir.dt.uint16
 ADD, MAX = mybir.AluOpType.add, mybir.AluOpType.max
-RELU = mybir.ActivationFunctionType.Relu
 
 P = 128
 TOKENS = 256
@@ -50,8 +49,8 @@ def tile_scatter_matmul_kernel(tc, base, x, w, b, offs, out):
                 stop=True,
             )
 
-        result = [held.tile([P, TOKENS], F32, name=f"result{i}") for i in range(SEQUENCES)]
-        nc.vector.tensor_scalar(result[0][:], window[0][:], bias[:, 0:1], 0.0, ADD, MAX)
-        nc.sync.dma_start(out[0], result[0][:])
-        nc.scalar.activation(result[1][:], window[1][:], RELU, bias=bias[:, 0:1])
-        nc.scalar.dma_start(out[1], result[1][:])
+        store_queues = [nc.sync, nc.scalar]
+        for i in range(SEQUENCES):
+            result = held.tile([P, TOKENS], F32, name=f"result{i}")
+            nc.vector.tensor_scalar(result[:], window[i][:], bias[:, 0:1], 0.0, ADD, MAX)
+            store_queues[i].dma_start(out[i], result[:])

@@ -25,12 +25,12 @@ def tile_scatter_matmul_kernel(tc, base, x, w, b, offs, out):
         base_tiles = [held.tile([P, TOKENS], BF16, name=f"base{i}") for i in range(SEQUENCES)]
         nc.scalar.dma_start(base_tiles[0][:], base[0])
         nc.sync.dma_start(base_tiles[1][:], base[1])
+        bias = held.tile([P, 1], F32, name="bias")
+        nc.scalar.dma_start(bias[:], b)
         weights = held.tile([P, P], BF16, name="weights")
         nc.scalar.dma_start(weights[:], w)
         moving = held.tile([P, ENTRIES], BF16, name="moving")
         nc.sync.dma_start(moving[:], x)
-        bias = held.tile([P, 1], F32, name="bias")
-        nc.scalar.dma_start(bias[:], b)
 
         identity = held.tile([P, P], BF16, name="identity")
         make_identity(nc, identity[:])

@@ -11,6 +11,8 @@ SEQUENCES = 2
 PIECE = ENTRIES // SEQUENCES
 PIECE_COLUMNS = PIECE // 16
 
+WARM_UP = 10
+
 FLOPS = 2 * P * P * ENTRIES
 
 
@@ -25,12 +27,18 @@ def tile_scatter_matmul_kernel(tc, base, x, w, b, offs, out):
         base_tiles = [held.tile([P, TOKENS], BF16, name=f"base{i}") for i in range(SEQUENCES)]
         nc.scalar.dma_start(base_tiles[0][:], base[0])
         nc.sync.dma_start(base_tiles[1][:], base[1])
-        bias = held.tile([P, 1], F32, name="bias")
-        nc.scalar.dma_start(bias[:], b)
         weights = held.tile([P, P], BF16, name="weights")
         nc.scalar.dma_start(weights[:], w)
         moving = held.tile([P, ENTRIES], BF16, name="moving")
         nc.sync.dma_start(moving[:], x)
+        bias = held.tile([P, 1], F32, name="bias")
+        nc.scalar.dma_start(bias[:], b)
+
+        zeros = held.tile([P, P], BF16, name="zeros")
+        nc.vector.memset(zeros[:], 0.0)
+        warm = windows.tile([P, P], F32, name="warm")
+        for repeat in range(WARM_UP):
+            nc.tensor.matmul(warm[:], zeros[:], zeros[:], start=True, stop=True)
 
         identity = held.tile([P, P], BF16, name="identity")
         make_identity(nc, identity[:])

@@ -3,6 +3,7 @@ from concourse.masks import make_identity
 
 BF16, F32, U16 = mybir.dt.bfloat16, mybir.dt.float32, mybir.dt.uint16
 ADD, MAX = mybir.AluOpType.add, mybir.AluOpType.max
+RELU = mybir.ActivationFunctionType.Relu
 
 P = 128
 TOKENS = 256
@@ -40,6 +41,9 @@ def tile_scatter_matmul_kernel(tc, base, x, w, b, offs, out):
         for repeat in range(WARM_UP):
             nc.tensor.matmul(warm[:], zeros[:], zeros[:], start=True, stop=True)
 
+        early = held.tile([P, 1], F32, name="early")
+        nc.scalar.activation(early[:], zeros[:, 0:1], RELU)
+
         identity = held.tile([P, P], BF16, name="identity")
         make_identity(nc, identity[:])
 
@@ -57,8 +61,8 @@ def tile_scatter_matmul_kernel(tc, base, x, w, b, offs, out):
                 stop=True,
             )
 
-        store_queues = [nc.sync, nc.scalar]
-        for i in range(SEQUENCES):
-            result = held.tile([P, TOKENS], F32, name=f"result{i}")
-            nc.vector.tensor_scalar(result[:], window[i][:], bias[:, 0:1], 0.0, ADD, MAX)
-            store_queues[i].dma_start(out[i], result[:])
+        result = [held.tile([P, TOKENS], F32, name=f"result{i}") for i in range(SEQUENCES)]
+        nc.scalar.activation(result[0][:], window[0][:], RELU, bias=bias[:, 0:1])
+        nc.scalar.dma_start(out[0], result[0][:])
+        nc.vector.tensor_scalar(result[1][:], window[1][:], bias[:, 0:1], 0.0, ADD, MAX)
+        nc.sync.dma_start(out[1], result[1][:])

import concourse.mybir as mybir
from concourse.masks import make_identity

BF16, F32, U16 = mybir.dt.bfloat16, mybir.dt.float32, mybir.dt.uint16
ADD, MAX = mybir.AluOpType.add, mybir.AluOpType.max
RELU = mybir.ActivationFunctionType.Relu

P = 128
TOKENS = 256
ENTRIES = 192
SEQUENCES = 2
PIECE = ENTRIES // SEQUENCES
PIECE_COLUMNS = PIECE // 16

WARM_UP = 10

FLOPS = 2 * P * P * ENTRIES


def tile_scatter_matmul_kernel(tc, base, x, w, b, offs, out):
    nc = tc.nc
    with (
        tc.tile_pool(name="held", bufs=1) as held,
        tc.psum_pool(name="windows", bufs=1) as windows,
    ):
        offsets = held.tile([P, ENTRIES // 16], U16, name="offsets")
        nc.sync.dma_start(offsets[:], offs)
        base_tiles = [held.tile([P, TOKENS], BF16, name=f"base{i}") for i in range(SEQUENCES)]
        nc.scalar.dma_start(base_tiles[0][:], base[0])
        nc.sync.dma_start(base_tiles[1][:], base[1])
        weights = held.tile([P, P], BF16, name="weights")
        nc.scalar.dma_start(weights[:], w)
        moving = held.tile([P, ENTRIES], BF16, name="moving")
        nc.sync.dma_start(moving[:], x)
        bias = held.tile([P, 1], F32, name="bias")
        nc.scalar.dma_start(bias[:], b)

        zeros = held.tile([P, P], BF16, name="zeros")
        nc.vector.memset(zeros[:], 0.0)
        warm = windows.tile([P, P], F32, name="warm")
        for repeat in range(WARM_UP):
            nc.tensor.matmul(warm[:], zeros[:], zeros[:], start=True, stop=True)

        early = held.tile([P, 1], F32, name="early")
        nc.scalar.activation(early[:], zeros[:, 0:1], RELU)

        identity = held.tile([P, P], BF16, name="identity")
        make_identity(nc, identity[:])

        window = [windows.tile([P, TOKENS], F32, name=f"window{i}") for i in range(SEQUENCES)]
        for i in range(SEQUENCES):
            nc.tensor.matmul(window[i][:], identity[:], base_tiles[i][:], start=True, stop=True)

        for i in range(SEQUENCES):
            piece = offsets[:, i * PIECE_COLUMNS : (i + 1) * PIECE_COLUMNS]
            nc.tensor.matmul(
                window[i][:].indirect(piece),
                weights[:],
                moving[:, i * PIECE : (i + 1) * PIECE],
                start=True,
                stop=True,
            )

        result = [held.tile([P, TOKENS], F32, name=f"result{i}") for i in range(SEQUENCES)]
        nc.scalar.activation(result[0][:], window[0][:], RELU, bias=bias[:, 0:1])
        nc.scalar.dma_start(out[0], result[0][:])
        nc.vector.tensor_scalar(result[1][:], window[1][:], bias[:, 0:1], 0.0, ADD, MAX)
        nc.sync.dma_start(out[1], result[1][:])
